import numpy as np
import ml_dtypes


def mxq(x, axis, fmt="e4m3"):
    dtype, down = {"e4m3": (ml_dtypes.float8_e4m3fn, 7), "e5m2": (ml_dtypes.float8_e5m2, 14)}[fmt]
    v = np.moveaxis(np.asarray(x, np.float32).astype(ml_dtypes.bfloat16).astype(np.float64), axis, -1)
    blocks = v.reshape(v.shape[:-1] + (-1, 32))
    amax = np.abs(blocks).max(-1, keepdims=True)
    byte = np.maximum(np.where(amax > 0, np.frexp(amax)[1] - 1 + 127, 0) - down, 1)
    scale = np.exp2(byte - 127.0)
    codes = (blocks / scale).astype(np.float32).astype(dtype).astype(np.float64)
    return np.moveaxis((codes * scale).reshape(v.shape), -1, axis)


WIDE = False


def mx_kscale(k):
    if not WIDE:
        return np.ones(k)
    levels = np.array([10, -10, 5, -5, 0])
    if k % 512:
        return np.exp2(np.random.permutation(np.resize(levels, k // 32))).repeat(32)
    a = np.empty((k // 512, 16))
    for p in range(k // 512):
        a[p, :8] = np.random.permutation(np.resize(levels, 8))
        for g in range(8):
            far = levels[np.abs(levels - a[p, g]) >= 10]
            a[p, g + 8] = far[np.random.randint(len(far))]
    return np.exp2(a.ravel()).repeat(32)


BF16 = ml_dtypes.bfloat16


def bf(x):
    return np.asarray(x, np.float32).astype(BF16)


def f64(x):
    return np.asarray(x).astype(np.float64)


E2M1 = np.array([0.0, 0.5, 1.0, 1.5, 2.0, 3.0, 4.0, 6.0, -0.0, -0.5, -1.0, -1.5, -2.0, -3.0, -4.0, -6.0])


def pack_weight(w, fmt):
    k, n = w.shape
    w = f64(bf(w)).reshape(k // 32, 32, n)
    amax = np.abs(w).max(1)
    if fmt == "e4m3":
        byte = np.frexp(amax)[1] - 1 + 127 - 7
    else:
        mant, ex = np.frexp(amax / 6.0)
        byte = np.where(mant > 0.5, ex, ex - 1) + 127
    byte = np.clip(np.where(amax > 0, byte, 1), 1, 254)
    scaled = (w * np.exp2(127.0 - byte)[:, None, :]).reshape(k, n).astype(np.float32)
    by_word = np.ascontiguousarray(scaled.reshape(k // 512, 128, 4, n).transpose(0, 1, 3, 2))
    if fmt == "e4m3":
        words = by_word.astype(ml_dtypes.float8_e4m3fn).view(np.uint8)
    else:
        c = by_word.astype(ml_dtypes.float4_e2m1fn).view(np.uint8) & 0xF
        words = c[..., 0::2] | (c[..., 1::2] << 4)
    return np.ascontiguousarray(words), np.ascontiguousarray(byte.astype(np.uint8).reshape(k // 512, 16, n))


def unpack_weight(words, scales, fmt):
    g, p, n, _ = words.shape
    if fmt == "e4m3":
        vals = np.ascontiguousarray(words).view(ml_dtypes.float8_e4m3fn).astype(np.float64)
    else:
        nib = np.empty((g, p, n, 4), np.uint8)
        nib[..., 0::2] = words & 0xF
        nib[..., 1::2] = words >> 4
        vals = E2M1[nib]
    vals = vals * np.repeat(np.exp2(scales.astype(np.float64) - 127.0), 8, axis=1)[..., None]
    return vals.transpose(0, 1, 3, 2).reshape(g * 512, n)
def pack4(w):
    words, scales = pack_weight(w, "e2m1")
    return words.reshape(words.shape[0], 128, -1), scales


def unpack4(words, scales):
    return unpack_weight(words.reshape(words.shape[0], 128, -1, 2), scales, "e2m1")


M, H, TD, TC, D = 1024, 4, 768, 256, 1024


def setup_inputs():
    a = np.exp(2.0 * np.random.standard_normal((M, H, TD + TC)))
    a = a / a.sum(axis=2, keepdims=True)
    a_doc = a[:, :, :TD].reshape(M, H * TD)
    a_chat = a[:, :, TD:].reshape(M, H * TC)
    u_doc = 2.0 * np.random.standard_normal((H * TD, D))
    u_chat = 2.0 * np.random.standard_normal((H * TC, D))
    s = mx_kscale(H * TD)
    t = mx_kscale(H * TC)
    u_doc_words, u_doc_scales = pack4(u_doc / s[:, None])
    return {"a_doc": bf(a_doc * s),
            "u_doc_words": u_doc_words,
            "u_doc_scales": u_doc_scales,
            "a_chat": bf(a_chat * t),
            "u_chat": bf(u_chat / t[:, None]),
            "bias": bf(0.3 * np.random.standard_normal(D)),
            "gain": bf(1.0 + 0.1 * np.random.standard_normal(D)),
            "x": bf(np.random.standard_normal((M, D)))}


def reference(a_doc, u_doc_words, u_doc_scales, a_chat, u_chat, bias, gain, x):
    ad = mxq(f64(a_doc), 1, "e4m3")
    ud = unpack4(u_doc_words, u_doc_scales)
    ac = mxq(f64(a_chat), 1, "e4m3")
    uc = mxq(f64(u_chat), 0, "e4m3")
    o = (ad @ ud) + (ac @ uc)
    return f64(x) + f64(gain) * (o + f64(bias))

@@ -1,0 +1,365 @@
+from contextlib import ExitStack
+
+import concourse.mybir as mybir
+from concourse.masks import make_identity
+
+F32 = mybir.dt.float32
+BF16 = mybir.dt.bfloat16
+I32 = mybir.dt.int32
+U32 = mybir.dt.uint32
+U8 = mybir.dt.uint8
+FP8X4 = mybir.dt.float8_e4m3fn_x4
+FP4X4 = mybir.dt.float4_e2m1fn_x4
+MULT = mybir.AluOpType.mult
+ADD = mybir.AluOpType.add
+
+P = 128
+M, D = 1024, 1024
+K_DOC, K_CHAT = 3072, 1024
+K_PASS = 512
+DOC_PASSES = K_DOC // K_PASS
+CHAT_PASSES = K_CHAT // K_PASS
+PASSES = DOC_PASSES + CHAT_PASSES
+TILES = M // P
+HALF = 512
+
+DVE_PREP = set()
+
+FLOPS = 2 * M * (K_DOC + K_CHAT) * D
+
+
+def tile_folded_value_attention_s1_kernel(
+    tc, a_doc, u_doc_words, u_doc_scales, a_chat, u_chat, bias, gain, x, out
+):
+    nc = tc.nc
+    with ExitStack() as ctx:
+        keep = ctx.enter_context(tc.tile_pool(name="keep", bufs=1))
+        raw = ctx.enter_context(tc.tile_pool(name="raw", bufs=TILES))
+        perm_pool = ctx.enter_context(tc.tile_pool(name="perm", bufs=2))
+        grp_pool = ctx.enter_context(tc.tile_pool(name="grp", bufs=2))
+        a_pool = ctx.enter_context(tc.tile_pool(name="aq", bufs=4))
+        ug_pool = ctx.enter_context(tc.tile_pool(name="ug", bufs=3))
+        x_pool = ctx.enter_context(tc.tile_pool(name="xp", bufs=4))
+        t_pool = ctx.enter_context(tc.tile_pool(name="tp", bufs=4))
+        psum = ctx.enter_context(tc.psum_pool(name="psum", bufs=1))
+        ctx.enter_context(tc.manual_schedule())
+
+        def bank(i, shape, dtype):
+            return psum.tile(shape, dtype, name="bank%d" % i, tag="bank%d" % i)
+
+        ident = keep.tile([P, P], F32, name="ident")
+        ident_bf = keep.tile([P, P], BF16, name="ident_bf")
+        vec = keep.tile([P, P], BF16, name="vec")
+        vcol = keep.tile([P, 16], BF16, name="vcol")
+        gain_b = keep.tile([P, D], BF16, name="gain_b")
+        gb = keep.tile([P, D], F32, name="gb")
+        ud = keep.tile([P, DOC_PASSES, 2 * D], U8, name="ud", align_bytes=256)
+        uds = keep.tile([P, DOC_PASSES * D], U8, name="uds", align_bytes=256)
+        uc_raw = [keep.tile([P, 4, D], BF16, name="uc_raw%d" % c) for c in range(CHAT_PASSES)]
+        uc = keep.tile([P, CHAT_PASSES, D], U32, name="uc", align_bytes=256)
+        ucs = keep.tile([P, CHAT_PASSES, D], U8, name="ucs", align_bytes=256)
+
+        nc.vector.memset(uds[:, 0 : 2 * D].bitcast(I32), 0)
+        nc.vector.memset(uds[:, 2 * D :].bitcast(I32), 0)
+        nc.vector.memset(vec[:], 0.0)
+        make_identity(nc, ident[:])
+        nc.vector.tensor_copy(out=ident_bf[:], in_=ident[:])
+
+        doc_raw = [raw.tile([P, K_DOC], BF16, name="doc%d" % m, tag="doc") for m in range(TILES)]
+        chat_raw = [raw.tile([P, K_CHAT], BF16, name="chat%d" % m, tag="chat") for m in range(TILES)]
+
+        def rows(m):
+            return slice(P * m, P * (m + 1))
+
+        def load_doc_piece(m, q):
+            cols = slice(1024 * q, 1024 * (q + 1))
+            nc.sync.dma_start(out=doc_raw[m][:, cols], in_=a_doc[rows(m), cols])
+
+        def load_doc(m):
+            nc.sync.dma_start(out=doc_raw[m][:], in_=a_doc[rows(m), :])
+
+        def load_chat(m):
+            nc.sync.dma_start(out=chat_raw[m][:], in_=a_chat[rows(m), :])
+
+        def load_ud(g, n):
+            nc.sync.dma_start(
+                out=ud[:, g : g + n, :].bitcast(I32),
+                in_=u_doc_words[g : g + n].rearrange("g p b -> p g b").bitcast(I32),
+            )
+
+        def load_uc(c):
+            nc.sync.dma_start(
+                out=uc_raw[c][:],
+                in_=u_chat[K_PASS * c : K_PASS * (c + 1), :].rearrange("(p j) n -> p j n", j=4),
+            )
+
+        x_t = {}
+
+        def load_x(m):
+            x_t[m] = x_pool.tile([P, D], BF16, name="x%d" % m, tag="x")
+            nc.sync.dma_start(out=x_t[m][:], in_=x[rows(m), :])
+
+        uds3 = uds[:].rearrange("p (g n) -> p g n", g=DOC_PASSES)
+
+        def load_uds(engine, g, n):
+            for q in range(4):
+                engine.dma_start(
+                    out=uds3[32 * q : 32 * q + 4, g : g + n].bitcast(I32),
+                    in_=u_doc_scales[g : g + n, 4 * q : 4 * q + 4, :].rearrange("g q n -> q g n").bitcast(I32),
+                )
+
+        load_doc_piece(0, 0)
+        load_ud(0, 2)
+        load_uds(nc.sync, 0, 2)
+        load_uds(nc.gpsimd, 2, 4)
+        nc.gpsimd.dma_start(out=vec[0:8, :], in_=gain.rearrange("(c n) -> c n", n=P))
+        nc.gpsimd.dma_start(out=vec[8:16, :], in_=bias.rearrange("(c n) -> c n", n=P))
+        load_doc_piece(0, 1)
+        load_ud(2, 2)
+        load_doc_piece(0, 2)
+        load_ud(4, 2)
+        for q in range(3):
+            load_doc_piece(1, q)
+        load_chat(0)
+        load_chat(1)
+        load_uc(0)
+        load_doc(2)
+        load_uc(1)
+        load_chat(2)
+        load_x(0)
+        load_doc(3)
+        load_chat(3)
+        load_x(1)
+        load_x(2)
+        for m in range(4, TILES):
+            load_doc(m)
+            load_chat(m)
+            load_x(m - 1)
+        load_x(TILES - 1)
+
+        perm = {}
+        grp = {}
+        codes = {}
+        scales = {}
+        tps = {}
+        acc = {}
+
+        def words(m, q):
+            if q < 3:
+                return doc_raw[m][:, 1024 * q : 1024 * (q + 1)].bitcast(F32)
+            return chat_raw[m][:].bitcast(F32)
+
+        def prep(m, q):
+            if q == 0:
+                perm[m] = perm_pool.tile([P, 4096], BF16, name="perm%d" % m, tag="perm")
+            copy = nc.vector.tensor_copy if (m, q) in DVE_PREP else nc.scalar.copy
+            copy(
+                out=perm[m][:, 1024 * q : 1024 * (q + 1)].bitcast(F32).rearrange("p (g u i) -> p g u i", g=2, u=2),
+                in_=words(m, q).rearrange("p (g i u) -> p g u i", g=2, u=2),
+            )
+
+        def transpose(m, q, b):
+            t = bank(b, [P, 4, P], F32)
+            tps[m, q] = t
+            for g in range(2):
+                for u in range(2):
+                    if m in perm:
+                        s = 512 * q + 256 * g + 128 * u
+                        src = perm[m][:].bitcast(F32)[:, s : s + 128]
+                    else:
+                        src = words(m, q)[:, 256 * g + u : 256 * (g + 1) : 2]
+                    nc.tensor.transpose(t[:, 2 * g + u, :], src, ident[:])
+
+        def evac(m, q):
+            if m not in grp:
+                grp[m] = grp_pool.tile([P, 4096], BF16, name="grp%d" % m, tag="grp", align_bytes=256)
+                codes[m] = a_pool.tile([P, PASSES * P], U32, name="ac%d" % m, tag="ac", align_bytes=256)
+                scales[m] = a_pool.tile([P, PASSES * P], U8, name="as%d" % m, tag="as", align_bytes=256)
+            nc.scalar.copy(
+                out=grp[m][:, 1024 * q : 1024 * (q + 1)].bitcast(F32).rearrange("p (g r u) -> p g r u", g=2, u=2),
+                in_=tps[m, q][:].rearrange("p (g u) r -> p g r u", u=2),
+            )
+
+        def quant(m, q, n=1):
+            w = slice(256 * q, 256 * (q + n))
+            nc.vector.quantize_mx(
+                out=codes[m][:, w].bitcast(FP8X4),
+                scales=scales[m][:, w],
+                in_=grp[m][:, 1024 * q : 1024 * (q + n)],
+            )
+
+        ug = {}
+
+        def uc_inter(engine, c, h):
+            t = ug_pool.tile([P, 4 * HALF], BF16, name="ug%d%d" % (c, h), tag="ug", align_bytes=256)
+            ug[c, h] = t
+            o = t[:].rearrange("p (c i t) -> p c t i", i=4, t=4)
+            i = uc_raw[c][:, :, HALF * h : HALF * (h + 1)].rearrange("p t (c i) -> p c t i", i=4)
+            if engine == "v":
+                nc.vector.tensor_copy(out=o, in_=i)
+            else:
+                nc.scalar.copy(out=o, in_=i)
+
+        def uc_quant(c, h):
+            w = slice(HALF * h, HALF * (h + 1))
+            nc.vector.quantize_mx(out=uc[:, c, w].bitcast(FP8X4), scales=ucs[:, c, w], in_=ug[c, h][:])
+
+        def open_acc(m, b):
+            for h in range(2):
+                acc[m, h] = bank(b + h, [P, HALF], F32)
+
+        def mm(m, g, h):
+            w = slice(P * g, P * (g + 1))
+            n = slice(HALF * h, HALF * (h + 1))
+            if g < DOC_PASSES:
+                rhs = ud[:, g, 2 * HALF * h : 2 * HALF * (h + 1)].bitcast(FP4X4)
+                rhs_scale = uds3[:, g, n]
+            else:
+                rhs = uc[:, g - DOC_PASSES, n].bitcast(FP8X4)
+                rhs_scale = ucs[:, g - DOC_PASSES, n]
+            nc.tensor.matmul_mx(
+                out=acc[m, h][:],
+                lhsT=codes[m][:, w].bitcast(FP8X4),
+                lhsT_scale=scales[m][:, w],
+                rhs=rhs,
+                rhs_scale=rhs_scale,
+                start=(g == 0),
+                stop=(g == PASSES - 1),
+            )
+
+        def mm_pass(m, g):
+            mm(m, g, 0)
+            mm(m, g, 1)
+
+        xb = {}
+
+        def residual(m):
+            xb[m] = keep.tile([P, D], F32, name="xb%d" % m)
+            for h in range(2):
+                n = slice(HALF * h, HALF * (h + 1))
+                nc.gpsimd.tensor_tensor(out=xb[m][:, n], in0=x_t[m][:, n], in1=gb[:, n], op=ADD)
+
+        scaled = {}
+
+        def epi_mul(m, h):
+            n = slice(HALF * h, HALF * (h + 1))
+            scaled[m, h] = t_pool.tile([P, HALF], F32, name="sc%d%d" % (m, h), tag="sc")
+            nc.vector.tensor_tensor(out=scaled[m, h][:], in0=acc[m, h][:], in1=gain_b[:, n], op=MULT)
+
+        def epi_add(m, h):
+            n = slice(HALF * h, HALF * (h + 1))
+            nc.vector.tensor_tensor(out=xb[m][:, n], in0=scaled[m, h][:], in1=xb[m][:, n], op=ADD)
+
+        def store(m):
+            nc.sync.dma_start(out=out[rows(m), :], in_=xb[m][:])
+
+        def store_half(m, h):
+            n = slice(HALF * h, HALF * (h + 1))
+            nc.sync.dma_start(out=out[rows(m), n], in_=xb[m][:, n])
+
+        transpose(0, 0, 6)
+        evac(0, 0)
+        quant(0, 0)
+        transpose(0, 1, 7)
+        evac(0, 1)
+        quant(0, 1)
+        open_acc(0, 0)
+        mm_pass(0, 0)
+        mm_pass(0, 1)
+        transpose(0, 2, 4)
+        evac(0, 2)
+        quant(0, 2)
+        mm_pass(0, 2)
+        mm_pass(0, 3)
+        for q, b in ((0, 5), (1, 6), (2, 7)):
+            transpose(1, q, b)
+            evac(1, q)
+            quant(1, q)
+        vt = bank(4, [P, P], BF16)
+        nc.tensor.transpose(vt[:], vec[:], ident_bf[:])
+        nc.vector.tensor_copy(out=vcol[:], in_=vt[:, 0:16])
+        mm_pass(0, 4)
+        mm_pass(0, 5)
+        uc_inter("v", 0, 0)
+        uc_inter("v", 0, 1)
+        uc_quant(0, 0)
+        uc_quant(0, 1)
+        for q in range(3):
+            prep(2, q)
+        open_acc(1, 2)
+        for g in range(6):
+            mm_pass(1, g)
+        transpose(0, 3, 5)
+        evac(0, 3)
+        quant(0, 3)
+        transpose(1, 3, 6)
+        evac(1, 3)
+        quant(1, 3)
+        prep(2, 3)
+        uc_inter("v", 1, 0)
+        mm_pass(0, 6)
+        mm_pass(1, 6)
+        for q, b in ((0, 7), (1, 5), (2, 6), (3, 7)):
+            transpose(2, q, b)
+            evac(2, q)
+        quant(2, 0)
+        quant(2, 1)
+        uc_inter("v", 1, 1)
+        quant(2, 2)
+        quant(2, 3)
+        uc_quant(1, 0)
+        uc_quant(1, 1)
+        gp = bank(5, [P, D], BF16)
+        bp = bank(6, [P, D], BF16)
+        for c in range(8):
+            nc.tensor.transpose(gp[:, P * c : P * (c + 1)], vcol[:, c : c + 1].to_broadcast([P, P]), ident_bf[:])
+        for c in range(8):
+            nc.tensor.transpose(bp[:, P * c : P * (c + 1)], vcol[:, 8 + c : 9 + c].to_broadcast([P, P]), ident_bf[:])
+        nc.scalar.copy(out=gain_b[:], in_=gp[:])
+        nc.vector.tensor_tensor(out=gb[:], in0=bp[:], in1=gain_b[:], op=MULT)
+        for q in range(4):
+            prep(3, q)
+        open_acc(2, 4)
+        for g in range(6):
+            mm_pass(2, g)
+        for m in range(2):
+            mm_pass(m, 7)
+        residual(0)
+        epi_mul(0, 0)
+        epi_mul(0, 1)
+        epi_add(0, 0)
+        epi_add(0, 1)
+        store(0)
+        residual(1)
+
+        for m in range(2, TILES):
+            nxt = m + 1
+            if nxt < TILES:
+                for q, b in ((0, 7), (1, 6), (2, 0), (3, 1)):
+                    transpose(nxt, q, b)
+                    evac(nxt, q)
+            if m + 2 < TILES:
+                for q in range(4):
+                    prep(m + 2, q)
+            epi_mul(m - 1, 0)
+            epi_mul(m - 1, 1)
+            if nxt < TILES:
+                quant(nxt, 0, 2)
+                quant(nxt, 2, 2)
+            epi_add(m - 1, 0)
+            epi_add(m - 1, 1)
+            store(m - 1)
+            residual(m)
+            if m == 2:
+                mm_pass(2, 6)
+                mm_pass(2, 7)
+            else:
+                open_acc(m, 4 if m % 2 == 0 else 2)
+                for h in range(2):
+                    for g in range(PASSES):
+                        mm(m, g, h)
+        last = TILES - 1
+        for h in range(2):
+            epi_mul(last, h)
+            epi_add(last, h)
+            store_half(last, h)

@@ -23,8 +23,6 @@ PASSES = DOC_PASSES + CHAT_PASSES
 TILES = M // P
 HALF = 512
 
-DVE_PREP = set()
-
 FLOPS = 2 * M * (K_DOC + K_CHAT) * D
 
 
@@ -52,6 +50,7 @@ def tile_folded_value_attention_s1_kernel(
         vec = keep.tile([P, P], BF16, name="vec")
         vcol = keep.tile([P, 16], BF16, name="vcol")
         gain_b = keep.tile([P, D], BF16, name="gain_b")
+        bias_b = keep.tile([P, D], BF16, name="bias_b")
         gb = keep.tile([P, D], F32, name="gb")
         ud = keep.tile([P, DOC_PASSES, 2 * D], U8, name="ud", align_bytes=256)
         uds = keep.tile([P, DOC_PASSES * D], U8, name="uds", align_bytes=256)
@@ -59,8 +58,7 @@ def tile_folded_value_attention_s1_kernel(
         uc = keep.tile([P, CHAT_PASSES, D], U32, name="uc", align_bytes=256)
         ucs = keep.tile([P, CHAT_PASSES, D], U8, name="ucs", align_bytes=256)
 
-        nc.vector.memset(uds[:, 0 : 2 * D].bitcast(I32), 0)
-        nc.vector.memset(uds[:, 2 * D :].bitcast(I32), 0)
+        nc.vector.memset(uds[:].bitcast(I32), 0)
         nc.vector.memset(vec[:], 0.0)
         make_identity(nc, ident[:])
         nc.vector.tensor_copy(out=ident_bf[:], in_=ident[:])
@@ -110,16 +108,15 @@ def tile_folded_value_attention_s1_kernel(
 
         load_doc_piece(0, 0)
         load_ud(0, 2)
-        load_uds(nc.sync, 0, 2)
-        load_uds(nc.gpsimd, 2, 4)
-        nc.gpsimd.dma_start(out=vec[0:8, :], in_=gain.rearrange("(c n) -> c n", n=P))
-        nc.gpsimd.dma_start(out=vec[8:16, :], in_=bias.rearrange("(c n) -> c n", n=P))
+        load_uds(nc.sync, 0, 6)
         load_doc_piece(0, 1)
         load_ud(2, 2)
         load_doc_piece(0, 2)
         load_ud(4, 2)
         for q in range(3):
             load_doc_piece(1, q)
+        nc.sync.dma_start(out=vec[0:8, :], in_=gain.rearrange("(c n) -> c n", n=P))
+        nc.sync.dma_start(out=vec[8:16, :], in_=bias.rearrange("(c n) -> c n", n=P))
         load_chat(0)
         load_chat(1)
         load_uc(0)
@@ -130,14 +127,14 @@ def tile_folded_value_attention_s1_kernel(
         load_doc(3)
         load_chat(3)
         load_x(1)
-        load_x(2)
         for m in range(4, TILES):
             load_doc(m)
             load_chat(m)
-            load_x(m - 1)
-        load_x(TILES - 1)
+            if m < 6:
+                load_x(m - 2)
 
         perm = {}
+        ready = set()
         grp = {}
         codes = {}
         scales = {}
@@ -150,10 +147,10 @@ def tile_folded_value_attention_s1_kernel(
             return chat_raw[m][:].bitcast(F32)
 
         def prep(m, q):
-            if q == 0:
+            ready.add((m, q))
+            if m not in perm:
                 perm[m] = perm_pool.tile([P, 4096], BF16, name="perm%d" % m, tag="perm")
-            copy = nc.vector.tensor_copy if (m, q) in DVE_PREP else nc.scalar.copy
-            copy(
+            nc.scalar.copy(
                 out=perm[m][:, 1024 * q : 1024 * (q + 1)].bitcast(F32).rearrange("p (g u i) -> p g u i", g=2, u=2),
                 in_=words(m, q).rearrange("p (g i u) -> p g u i", g=2, u=2),
             )
@@ -163,7 +160,7 @@ def tile_folded_value_attention_s1_kernel(
             tps[m, q] = t
             for g in range(2):
                 for u in range(2):
-                    if m in perm:
+                    if (m, q) in ready:
                         s = 512 * q + 256 * g + 128 * u
                         src = perm[m][:].bitcast(F32)[:, s : s + 128]
                     else:
@@ -227,6 +224,34 @@ def tile_folded_value_attention_s1_kernel(
                 stop=(g == PASSES - 1),
             )
 
+        def tail_mm(m, c, b):
+            t = bank(b, [P, P], F32)
+            acc[m, "t", c] = t
+            n = slice(HALF + P * c, HALF + P * (c + 1))
+            for g in range(PASSES):
+                w = slice(P * g, P * (g + 1))
+                if g < DOC_PASSES:
+                    rhs = ud[:, g, 2 * n.start : 2 * n.stop].bitcast(FP4X4)
+                    rhs_scale = uds3[:, g, n]
+                else:
+                    rhs = uc[:, g - DOC_PASSES, n].bitcast(FP8X4)
+                    rhs_scale = ucs[:, g - DOC_PASSES, n]
+                nc.tensor.matmul_mx(
+                    out=t[:],
+                    lhsT=codes[m][:, w].bitcast(FP8X4),
+                    lhsT_scale=scales[m][:, w],
+                    rhs=rhs,
+                    rhs_scale=rhs_scale,
+                    start=(g == 0),
+                    stop=(g == PASSES - 1),
+                )
+
+        def tail_epi(m, c):
+            n = slice(HALF + P * c, HALF + P * (c + 1))
+            t = t_pool.tile([P, HALF], F32, name="st%d" % c, tag="sc")
+            nc.vector.tensor_tensor(out=t[:, 0:P], in0=acc[m, "t", c][:], in1=gain_b[:, n], op=MULT)
+            nc.vector.tensor_tensor(out=xb[m][:, n], in0=t[:, 0:P], in1=xb[m][:, n], op=ADD)
+
         def mm_pass(m, g):
             mm(m, g, 0)
             mm(m, g, 1)
@@ -280,23 +305,27 @@ def tile_folded_value_attention_s1_kernel(
         nc.vector.tensor_copy(out=vcol[:], in_=vt[:, 0:16])
         mm_pass(0, 4)
         mm_pass(0, 5)
+        prep(0, 3)
+        prep(1, 3)
         uc_inter("v", 0, 0)
-        uc_inter("v", 0, 1)
+        uc_inter("s", 0, 1)
         uc_quant(0, 0)
-        uc_quant(0, 1)
-        for q in range(3):
-            prep(2, q)
         open_acc(1, 2)
-        for g in range(6):
-            mm_pass(1, g)
+        mm_pass(1, 0)
+        mm_pass(1, 1)
         transpose(0, 3, 5)
         evac(0, 3)
-        quant(0, 3)
         transpose(1, 3, 6)
         evac(1, 3)
+        quant(0, 3)
         quant(1, 3)
-        prep(2, 3)
+        for g in range(2, 6):
+            mm_pass(1, g)
+        uc_quant(0, 1)
+        for q in range(4):
+            prep(2, q)
         uc_inter("v", 1, 0)
+        uc_inter("v", 1, 1)
         mm_pass(0, 6)
         mm_pass(1, 6)
         for q, b in ((0, 7), (1, 5), (2, 6), (3, 7)):
@@ -304,29 +333,31 @@ def tile_folded_value_attention_s1_kernel(
             evac(2, q)
         quant(2, 0)
         quant(2, 1)
-        uc_inter("v", 1, 1)
-        quant(2, 2)
-        quant(2, 3)
         uc_quant(1, 0)
+        quant(2, 2)
         uc_quant(1, 1)
+        quant(2, 3)
         gp = bank(5, [P, D], BF16)
-        bp = bank(6, [P, D], BF16)
         for c in range(8):
             nc.tensor.transpose(gp[:, P * c : P * (c + 1)], vcol[:, c : c + 1].to_broadcast([P, P]), ident_bf[:])
+        bp = bank(6, [P, D], BF16)
         for c in range(8):
             nc.tensor.transpose(bp[:, P * c : P * (c + 1)], vcol[:, 8 + c : 9 + c].to_broadcast([P, P]), ident_bf[:])
         nc.scalar.copy(out=gain_b[:], in_=gp[:])
-        nc.vector.tensor_tensor(out=gb[:], in0=bp[:], in1=gain_b[:], op=MULT)
+        nc.scalar.copy(out=bias_b[:], in_=bp[:])
+        nc.gpsimd.tensor_tensor(out=gb[:], in0=gain_b[:], in1=bias_b[:], op=MULT)
         for q in range(4):
             prep(3, q)
+        for m in range(2):
+            mm_pass(m, 7)
         open_acc(2, 4)
         for g in range(6):
             mm_pass(2, g)
-        for m in range(2):
-            mm_pass(m, 7)
         residual(0)
         epi_mul(0, 0)
         epi_mul(0, 1)
+        epi_mul(1, 0)
+        epi_mul(1, 1)
         epi_add(0, 0)
         epi_add(0, 1)
         store(0)
@@ -341,25 +372,37 @@ def tile_folded_value_attention_s1_kernel(
             if m + 2 < TILES:
                 for q in range(4):
                     prep(m + 2, q)
-            epi_mul(m - 1, 0)
-            epi_mul(m - 1, 1)
+            if m > 2:
+                epi_mul(m - 1, 0)
+                epi_mul(m - 1, 1)
             if nxt < TILES:
                 quant(nxt, 0, 2)
                 quant(nxt, 2, 2)
             epi_add(m - 1, 0)
             epi_add(m - 1, 1)
             store(m - 1)
+            if m < 6:
+                load_x(m + 2)
             residual(m)
             if m == 2:
                 mm_pass(2, 6)
                 mm_pass(2, 7)
-            else:
+            elif nxt < TILES:
                 open_acc(m, 4 if m % 2 == 0 else 2)
                 for h in range(2):
                     for g in range(PASSES):
                         mm(m, g, h)
         last = TILES - 1
-        for h in range(2):
-            epi_mul(last, h)
-            epi_add(last, h)
-            store_half(last, h)
+        open_acc(last, 2)
+        for g in range(PASSES):
+            mm(last, g, 0)
+        epi_mul(last, 0)
+        epi_add(last, 0)
+        store_half(last, 0)
+        for c, b in enumerate((0, 1, 6, 7)):
+            tail_mm(last, c, b)
+        for c in range(4):
+            tail_epi(last, c)
+            if c == 2:
+                nc.sync.dma_start(out=out[rows(last), HALF : HALF + 3 * P], in_=xb[last][:, HALF : HALF + 3 * P])
+        nc.sync.dma_start(out=out[rows(last), D - P :], in_=xb[last][:, D - P :])

@@ -37,8 +37,9 @@ def tile_folded_value_attention_s1_kernel(
         grp_pool = ctx.enter_context(tc.tile_pool(name="grp", bufs=2))
         a_pool = ctx.enter_context(tc.tile_pool(name="aq", bufs=4))
         ug_pool = ctx.enter_context(tc.tile_pool(name="ug", bufs=3))
-        x_pool = ctx.enter_context(tc.tile_pool(name="xp", bufs=4))
-        t_pool = ctx.enter_context(tc.tile_pool(name="tp", bufs=4))
+        x_pool = ctx.enter_context(tc.tile_pool(name="xp", bufs=8))
+        xb_pool = ctx.enter_context(tc.tile_pool(name="xbp", bufs=4))
+        t_pool = ctx.enter_context(tc.tile_pool(name="tp", bufs=2))
         psum = ctx.enter_context(tc.psum_pool(name="psum", bufs=1))
         ctx.enter_context(tc.manual_schedule())
 
@@ -58,7 +59,8 @@ def tile_folded_value_attention_s1_kernel(
         uc = keep.tile([P, CHAT_PASSES, D], U32, name="uc", align_bytes=256)
         ucs = keep.tile([P, CHAT_PASSES, D], U8, name="ucs", align_bytes=256)
 
-        nc.vector.memset(uds[:].bitcast(I32), 0)
+        nc.vector.memset(uds[:, 0 : 2 * D].bitcast(I32), 0)
+        nc.vector.memset(uds[:, 2 * D :].bitcast(I32), 0)
         nc.vector.memset(vec[:], 0.0)
         make_identity(nc, ident[:])
         nc.vector.tensor_copy(out=ident_bf[:], in_=ident[:])
@@ -107,31 +109,11 @@ def tile_folded_value_attention_s1_kernel(
                 )
 
         load_doc_piece(0, 0)
+        load_uds(nc.sync, 0, 2)
         load_ud(0, 2)
-        load_uds(nc.sync, 0, 6)
         load_doc_piece(0, 1)
         load_ud(2, 2)
         load_doc_piece(0, 2)
-        load_ud(4, 2)
-        for q in range(3):
-            load_doc_piece(1, q)
-        nc.sync.dma_start(out=vec[0:8, :], in_=gain.rearrange("(c n) -> c n", n=P))
-        nc.sync.dma_start(out=vec[8:16, :], in_=bias.rearrange("(c n) -> c n", n=P))
-        load_chat(0)
-        load_chat(1)
-        load_uc(0)
-        load_doc(2)
-        load_uc(1)
-        load_chat(2)
-        load_x(0)
-        load_doc(3)
-        load_chat(3)
-        load_x(1)
-        for m in range(4, TILES):
-            load_doc(m)
-            load_chat(m)
-            if m < 6:
-                load_x(m - 2)
 
         perm = {}
         ready = set()
@@ -248,9 +230,9 @@ def tile_folded_value_attention_s1_kernel(
 
         def tail_epi(m, c):
             n = slice(HALF + P * c, HALF + P * (c + 1))
-            t = t_pool.tile([P, HALF], F32, name="st%d" % c, tag="sc")
-            nc.vector.tensor_tensor(out=t[:, 0:P], in0=acc[m, "t", c][:], in1=gain_b[:, n], op=MULT)
-            nc.vector.tensor_tensor(out=xb[m][:, n], in0=t[:, 0:P], in1=xb[m][:, n], op=ADD)
+            t = scaled[m]
+            nc.vector.tensor_tensor(out=t[:, n], in0=acc[m, "t", c][:], in1=gain_b[:, n], op=MULT)
+            nc.vector.tensor_tensor(out=xb[m][:, n], in0=t[:, n], in1=xb[m][:, n], op=ADD)
 
         def mm_pass(m, g):
             mm(m, g, 0)
@@ -259,21 +241,20 @@ def tile_folded_value_attention_s1_kernel(
         xb = {}
 
         def residual(m):
-            xb[m] = keep.tile([P, D], F32, name="xb%d" % m)
-            for h in range(2):
-                n = slice(HALF * h, HALF * (h + 1))
-                nc.gpsimd.tensor_tensor(out=xb[m][:, n], in0=x_t[m][:, n], in1=gb[:, n], op=ADD)
+            xb[m] = xb_pool.tile([P, D], F32, name="xb%d" % m, tag="xb")
+            nc.vector.tensor_tensor(out=xb[m][:], in0=x_t[m][:], in1=gb[:], op=ADD)
 
         scaled = {}
 
         def epi_mul(m, h):
             n = slice(HALF * h, HALF * (h + 1))
-            scaled[m, h] = t_pool.tile([P, HALF], F32, name="sc%d%d" % (m, h), tag="sc")
-            nc.vector.tensor_tensor(out=scaled[m, h][:], in0=acc[m, h][:], in1=gain_b[:, n], op=MULT)
+            if h == 0:
+                scaled[m] = t_pool.tile([P, D], F32, name="sc%d" % m, tag="sc")
+            nc.vector.tensor_tensor(out=scaled[m][:, n], in0=acc[m, h][:], in1=gain_b[:, n], op=MULT)
 
-        def epi_add(m, h):
-            n = slice(HALF * h, HALF * (h + 1))
-            nc.vector.tensor_tensor(out=xb[m][:, n], in0=scaled[m, h][:], in1=xb[m][:, n], op=ADD)
+        def epi_add(m, h0=0, h1=2):
+            n = slice(HALF * h0, HALF * h1)
+            nc.vector.tensor_tensor(out=xb[m][:, n], in0=scaled[m][:, n], in1=xb[m][:, n], op=ADD)
 
         def store(m):
             nc.sync.dma_start(out=out[rows(m), :], in_=xb[m][:])
@@ -285,6 +266,28 @@ def tile_folded_value_attention_s1_kernel(
         transpose(0, 0, 6)
         evac(0, 0)
         quant(0, 0)
+        load_uds(nc.scalar, 2, 4)
+        load_ud(4, 2)
+        for q in range(3):
+            load_doc_piece(1, q)
+        nc.sync.dma_start(out=vec[0:8, :], in_=gain.rearrange("(c n) -> c n", n=P))
+        nc.sync.dma_start(out=vec[8:16, :], in_=bias.rearrange("(c n) -> c n", n=P))
+        load_chat(0)
+        load_chat(1)
+        load_uc(0)
+        load_doc(2)
+        load_uc(1)
+        load_chat(2)
+        load_x(0)
+        load_doc(3)
+        load_chat(3)
+        load_x(1)
+        for m in range(4, TILES):
+            load_doc(m)
+            load_chat(m)
+            load_x(m - 2)
+        load_x(6)
+        load_x(7)
         transpose(0, 1, 7)
         evac(0, 1)
         quant(0, 1)
@@ -345,7 +348,6 @@ def tile_folded_value_attention_s1_kernel(
             nc.tensor.transpose(bp[:, P * c : P * (c + 1)], vcol[:, 8 + c : 9 + c].to_broadcast([P, P]), ident_bf[:])
         nc.scalar.copy(out=gain_b[:], in_=gp[:])
         nc.scalar.copy(out=bias_b[:], in_=bp[:])
-        nc.gpsimd.tensor_tensor(out=gb[:], in0=gain_b[:], in1=bias_b[:], op=MULT)
         for q in range(4):
             prep(3, q)
         for m in range(2):
@@ -353,18 +355,21 @@ def tile_folded_value_attention_s1_kernel(
         open_acc(2, 4)
         for g in range(6):
             mm_pass(2, g)
-        residual(0)
         epi_mul(0, 0)
         epi_mul(0, 1)
         epi_mul(1, 0)
         epi_mul(1, 1)
-        epi_add(0, 0)
-        epi_add(0, 1)
+        nc.vector.tensor_tensor(out=gb[:], in0=gain_b[:], in1=bias_b[:], op=MULT)
+        residual(0)
+        epi_add(0)
         store(0)
         residual(1)
 
         for m in range(2, TILES):
             nxt = m + 1
+            if m > 2:
+                epi_mul(m - 1, 0)
+                epi_mul(m - 1, 1)
             if nxt < TILES:
                 for q, b in ((0, 7), (1, 6), (2, 0), (3, 1)):
                     transpose(nxt, q, b)
@@ -372,18 +377,20 @@ def tile_folded_value_attention_s1_kernel(
             if m + 2 < TILES:
                 for q in range(4):
                     prep(m + 2, q)
-            if m > 2:
-                epi_mul(m - 1, 0)
-                epi_mul(m - 1, 1)
-            if nxt < TILES:
+            if m == 2:
                 quant(nxt, 0, 2)
                 quant(nxt, 2, 2)
-            epi_add(m - 1, 0)
-            epi_add(m - 1, 1)
+                residual(m)
+                epi_add(m - 1)
+                residual(nxt)
+            else:
+                if nxt < TILES:
+                    residual(nxt)
+                epi_add(m - 1)
+                if nxt < TILES:
+                    quant(nxt, 0, 2)
+                    quant(nxt, 2, 2)
             store(m - 1)
-            if m < 6:
-                load_x(m + 2)
-            residual(m)
             if m == 2:
                 mm_pass(2, 6)
                 mm_pass(2, 7)
@@ -397,7 +404,7 @@ def tile_folded_value_attention_s1_kernel(
         for g in range(PASSES):
             mm(last, g, 0)
         epi_mul(last, 0)
-        epi_add(last, 0)
+        epi_add(last, 0, 1)
         store_half(last, 0)
         for c, b in enumerate((0, 1, 6, 7)):
             tail_mm(last, c, b)

@@ -33,7 +33,7 @@ def tile_folded_value_attention_s1_kernel(
     with ExitStack() as ctx:
         keep = ctx.enter_context(tc.tile_pool(name="keep", bufs=1))
         raw = ctx.enter_context(tc.tile_pool(name="raw", bufs=TILES))
-        perm_pool = ctx.enter_context(tc.tile_pool(name="perm", bufs=2))
+        perm_pool = ctx.enter_context(tc.tile_pool(name="perm", bufs=3))
         grp_pool = ctx.enter_context(tc.tile_pool(name="grp", bufs=2))
         a_pool = ctx.enter_context(tc.tile_pool(name="aq", bufs=4))
         ug_pool = ctx.enter_context(tc.tile_pool(name="ug", bufs=3))
@@ -51,7 +51,6 @@ def tile_folded_value_attention_s1_kernel(
         vec = keep.tile([P, P], BF16, name="vec")
         vcol = keep.tile([P, 16], BF16, name="vcol")
         gain_b = keep.tile([P, D], BF16, name="gain_b")
-        bias_b = keep.tile([P, D], BF16, name="bias_b")
         gb = keep.tile([P, D], F32, name="gb")
         ud = keep.tile([P, DOC_PASSES, 2 * D], U8, name="ud", align_bytes=256)
         uds = keep.tile([P, DOC_PASSES * D], U8, name="uds", align_bytes=256)
@@ -59,8 +58,7 @@ def tile_folded_value_attention_s1_kernel(
         uc = keep.tile([P, CHAT_PASSES, D], U32, name="uc", align_bytes=256)
         ucs = keep.tile([P, CHAT_PASSES, D], U8, name="ucs", align_bytes=256)
 
-        nc.vector.memset(uds[:, 0 : 2 * D].bitcast(I32), 0)
-        nc.vector.memset(uds[:, 2 * D :].bitcast(I32), 0)
+        nc.vector.memset(uds[:].bitcast(I32), 0)
         nc.vector.memset(vec[:], 0.0)
         make_identity(nc, ident[:])
         nc.vector.tensor_copy(out=ident_bf[:], in_=ident[:])
@@ -71,8 +69,8 @@ def tile_folded_value_attention_s1_kernel(
         def rows(m):
             return slice(P * m, P * (m + 1))
 
-        def load_doc_piece(m, q):
-            cols = slice(1024 * q, 1024 * (q + 1))
+        def load_doc_piece(m, q, n=1):
+            cols = slice(1024 * q, 1024 * (q + n))
             nc.sync.dma_start(out=doc_raw[m][:, cols], in_=a_doc[rows(m), cols])
 
         def load_doc(m):
@@ -101,19 +99,40 @@ def tile_folded_value_attention_s1_kernel(
 
         uds3 = uds[:].rearrange("p (g n) -> p g n", g=DOC_PASSES)
 
-        def load_uds(engine, g, n):
-            for q in range(4):
-                engine.dma_start(
-                    out=uds3[32 * q : 32 * q + 4, g : g + n].bitcast(I32),
-                    in_=u_doc_scales[g : g + n, 4 * q : 4 * q + 4, :].rearrange("g q n -> q g n").bitcast(I32),
+        def load_uds(g, n):
+            for r in range(4):
+                nc.sync.dma_start(
+                    out=uds3[r:P:32, g : g + n].bitcast(I32),
+                    in_=u_doc_scales[g : g + n].rearrange("g (q r) n -> r q g n", r=4)[r].bitcast(I32),
                 )
 
         load_doc_piece(0, 0)
-        load_uds(nc.sync, 0, 2)
         load_ud(0, 2)
+        load_uds(0, 6)
         load_doc_piece(0, 1)
         load_ud(2, 2)
         load_doc_piece(0, 2)
+        load_ud(4, 2)
+        for q in range(3):
+            load_doc_piece(1, q)
+        nc.sync.dma_start(out=vec[0:8, :], in_=gain.rearrange("(c n) -> c n", n=P))
+        nc.sync.dma_start(out=vec[8:16, :], in_=bias.rearrange("(c n) -> c n", n=P))
+        load_chat(0)
+        load_chat(1)
+        load_uc(0)
+        load_doc(2)
+        load_uc(1)
+        load_chat(2)
+        load_x(0)
+        load_doc(3)
+        load_chat(3)
+        load_x(1)
+        for m in range(4, TILES):
+            load_doc(m)
+            load_chat(m)
+            load_x(m - 2)
+        load_x(6)
+        load_x(7)
 
         perm = {}
         ready = set()
@@ -169,15 +188,17 @@ def tile_folded_value_attention_s1_kernel(
 
         ug = {}
 
-        def uc_inter(engine, c, h):
-            t = ug_pool.tile([P, 4 * HALF], BF16, name="ug%d%d" % (c, h), tag="ug", align_bytes=256)
-            ug[c, h] = t
-            o = t[:].rearrange("p (c i t) -> p c t i", i=4, t=4)
-            i = uc_raw[c][:, :, HALF * h : HALF * (h + 1)].rearrange("p t (c i) -> p c t i", i=4)
-            if engine == "v":
-                nc.vector.tensor_copy(out=o, in_=i)
-            else:
-                nc.scalar.copy(out=o, in_=i)
+        def uc_inter(engine, c, quarters):
+            for quarter in quarters:
+                h, part = divmod(quarter, 2)
+                if (c, h) not in ug:
+                    ug[c, h] = ug_pool.tile([P, 4 * HALF], BF16, name="ug%d%d" % (c, h), tag="ug", align_bytes=256)
+                o = ug[c, h][:, 1024 * part : 1024 * (part + 1)].rearrange("p (c i t) -> p c t i", i=4, t=4)
+                i = uc_raw[c][:, :, 256 * quarter : 256 * (quarter + 1)].rearrange("p t (c i) -> p c t i", i=4)
+                if engine == "v":
+                    nc.vector.tensor_copy(out=o, in_=i)
+                else:
+                    nc.scalar.copy(out=o, in_=i)
 
         def uc_quant(c, h):
             w = slice(HALF * h, HALF * (h + 1))
@@ -266,37 +287,13 @@ def tile_folded_value_attention_s1_kernel(
         transpose(0, 0, 6)
         evac(0, 0)
         quant(0, 0)
-        load_uds(nc.scalar, 2, 4)
-        load_ud(4, 2)
-        for q in range(3):
-            load_doc_piece(1, q)
-        nc.sync.dma_start(out=vec[0:8, :], in_=gain.rearrange("(c n) -> c n", n=P))
-        nc.sync.dma_start(out=vec[8:16, :], in_=bias.rearrange("(c n) -> c n", n=P))
-        load_chat(0)
-        load_chat(1)
-        load_uc(0)
-        load_doc(2)
-        load_uc(1)
-        load_chat(2)
-        load_x(0)
-        load_doc(3)
-        load_chat(3)
-        load_x(1)
-        for m in range(4, TILES):
-            load_doc(m)
-            load_chat(m)
-            load_x(m - 2)
-        load_x(6)
-        load_x(7)
-        transpose(0, 1, 7)
-        evac(0, 1)
-        quant(0, 1)
         open_acc(0, 0)
         mm_pass(0, 0)
+        for q, b in ((1, 7), (2, 4)):
+            transpose(0, q, b)
+            evac(0, q)
+            quant(0, q)
         mm_pass(0, 1)
-        transpose(0, 2, 4)
-        evac(0, 2)
-        quant(0, 2)
         mm_pass(0, 2)
         mm_pass(0, 3)
         for q, b in ((0, 5), (1, 6), (2, 7)):
@@ -310,9 +307,6 @@ def tile_folded_value_attention_s1_kernel(
         mm_pass(0, 5)
         prep(0, 3)
         prep(1, 3)
-        uc_inter("v", 0, 0)
-        uc_inter("s", 0, 1)
-        uc_quant(0, 0)
         open_acc(1, 2)
         mm_pass(1, 0)
         mm_pass(1, 1)
@@ -320,25 +314,30 @@ def tile_folded_value_attention_s1_kernel(
         evac(0, 3)
         transpose(1, 3, 6)
         evac(1, 3)
+        uc_inter("v", 0, (0, 1))
+        uc_inter("s", 0, (3,))
         quant(0, 3)
+        uc_inter("v", 0, (2,))
         quant(1, 3)
+        uc_quant(0, 0)
+        uc_quant(0, 1)
         for g in range(2, 6):
             mm_pass(1, g)
-        uc_quant(0, 1)
         for q in range(4):
             prep(2, q)
-        uc_inter("v", 1, 0)
-        uc_inter("v", 1, 1)
-        mm_pass(0, 6)
-        mm_pass(1, 6)
+        uc_inter("v", 1, (0, 1))
+        for h in range(2):
+            for m in range(2):
+                mm(m, 6, h)
         for q, b in ((0, 7), (1, 5), (2, 6), (3, 7)):
             transpose(2, q, b)
             evac(2, q)
         quant(2, 0)
-        quant(2, 1)
         uc_quant(1, 0)
-        quant(2, 2)
+        uc_inter("v", 1, (2, 3))
+        quant(2, 1)
         uc_quant(1, 1)
+        quant(2, 2)
         quant(2, 3)
         gp = bank(5, [P, D], BF16)
         for c in range(8):
@@ -347,11 +346,14 @@ def tile_folded_value_attention_s1_kernel(
         for c in range(8):
             nc.tensor.transpose(bp[:, P * c : P * (c + 1)], vcol[:, 8 + c : 9 + c].to_broadcast([P, P]), ident_bf[:])
         nc.scalar.copy(out=gain_b[:], in_=gp[:])
-        nc.scalar.copy(out=bias_b[:], in_=bp[:])
+        nc.vector.tensor_tensor(out=gb[:], in0=bp[:], in1=gain_b[:], op=MULT)
         for q in range(4):
             prep(3, q)
-        for m in range(2):
-            mm_pass(m, 7)
+        for q in range(4):
+            prep(4, q)
+        for h in range(2):
+            for m in range(2):
+                mm(m, 7, h)
         open_acc(2, 4)
         for g in range(6):
             mm_pass(2, g)
@@ -359,7 +361,6 @@ def tile_folded_value_attention_s1_kernel(
         epi_mul(0, 1)
         epi_mul(1, 0)
         epi_mul(1, 1)
-        nc.vector.tensor_tensor(out=gb[:], in0=gain_b[:], in1=bias_b[:], op=MULT)
         residual(0)
         epi_add(0)
         store(0)
@@ -374,13 +375,14 @@ def tile_folded_value_attention_s1_kernel(
                 for q, b in ((0, 7), (1, 6), (2, 0), (3, 1)):
                     transpose(nxt, q, b)
                     evac(nxt, q)
-            if m + 2 < TILES:
+            if m + 3 < TILES:
                 for q in range(4):
-                    prep(m + 2, q)
-            if m == 2:
+                    prep(m + 3, q)
+            if m < 4:
                 quant(nxt, 0, 2)
                 quant(nxt, 2, 2)
-                residual(m)
+                if m == 2:
+                    residual(m)
                 epi_add(m - 1)
                 residual(nxt)
             else:

@@ -16,12 +16,22 @@ ADD = mybir.AluOpType.add
 P = 128
 M, D = 1024, 1024
 K_DOC, K_CHAT = 3072, 1024
-K_PASS = 512
+PACK = 4
+K_PASS = P * PACK
 DOC_PASSES = K_DOC // K_PASS
 CHAT_PASSES = K_CHAT // K_PASS
 PASSES = DOC_PASSES + CHAT_PASSES
 TILES = M // P
+
+SLICE = 2 * K_PASS
+SLICE_WORDS = SLICE // 2
+SLICES = (K_DOC + K_CHAT) // SLICE
+CHAT_SLICE = SLICES - 1
+
 HALF = 512
+HALVES = (slice(0, HALF), slice(HALF, D))
+QUARTER = HALF // 2
+VEC_ROWS = D // P
 
 FLOPS = 2 * M * (K_DOC + K_CHAT) * D
 
@@ -32,45 +42,48 @@ def tile_folded_value_attention_s1_kernel(
     nc = tc.nc
     with ExitStack() as ctx:
         keep = ctx.enter_context(tc.tile_pool(name="keep", bufs=1))
-        raw = ctx.enter_context(tc.tile_pool(name="raw", bufs=TILES))
-        perm_pool = ctx.enter_context(tc.tile_pool(name="perm", bufs=3))
-        grp_pool = ctx.enter_context(tc.tile_pool(name="grp", bufs=2))
-        a_pool = ctx.enter_context(tc.tile_pool(name="aq", bufs=4))
-        ug_pool = ctx.enter_context(tc.tile_pool(name="ug", bufs=3))
-        x_pool = ctx.enter_context(tc.tile_pool(name="xp", bufs=8))
-        xb_pool = ctx.enter_context(tc.tile_pool(name="xbp", bufs=4))
-        t_pool = ctx.enter_context(tc.tile_pool(name="tp", bufs=2))
+        doc_pool = ctx.enter_context(tc.tile_pool(name="doc", bufs=TILES))
+        chat_pool = ctx.enter_context(tc.tile_pool(name="chat", bufs=TILES))
+        x_pool = ctx.enter_context(tc.tile_pool(name="x", bufs=TILES))
+        order_pool = ctx.enter_context(tc.tile_pool(name="order", bufs=3))
+        grouped_pool = ctx.enter_context(tc.tile_pool(name="grouped", bufs=3))
+        code_pool = ctx.enter_context(tc.tile_pool(name="codes", bufs=4))
+        u_grouped_pool = ctx.enter_context(tc.tile_pool(name="u_grouped", bufs=3))
+        residual_pool = ctx.enter_context(tc.tile_pool(name="residual", bufs=4))
+        scaled_pool = ctx.enter_context(tc.tile_pool(name="scaled", bufs=2))
         psum = ctx.enter_context(tc.psum_pool(name="psum", bufs=1))
         ctx.enter_context(tc.manual_schedule())
 
         def bank(i, shape, dtype):
             return psum.tile(shape, dtype, name="bank%d" % i, tag="bank%d" % i)
 
-        ident = keep.tile([P, P], F32, name="ident")
-        ident_bf = keep.tile([P, P], BF16, name="ident_bf")
-        vec = keep.tile([P, P], BF16, name="vec")
-        vcol = keep.tile([P, 16], BF16, name="vcol")
-        gain_b = keep.tile([P, D], BF16, name="gain_b")
-        gb = keep.tile([P, D], F32, name="gb")
-        ud = keep.tile([P, DOC_PASSES, 2 * D], U8, name="ud", align_bytes=256)
-        uds = keep.tile([P, DOC_PASSES * D], U8, name="uds", align_bytes=256)
-        uc_raw = [keep.tile([P, 4, D], BF16, name="uc_raw%d" % c) for c in range(CHAT_PASSES)]
-        uc = keep.tile([P, CHAT_PASSES, D], U32, name="uc", align_bytes=256)
-        ucs = keep.tile([P, CHAT_PASSES, D], U8, name="ucs", align_bytes=256)
-
-        nc.vector.memset(uds[:].bitcast(I32), 0)
-        nc.vector.memset(vec[:], 0.0)
-        make_identity(nc, ident[:])
-        nc.vector.tensor_copy(out=ident_bf[:], in_=ident[:])
-
-        doc_raw = [raw.tile([P, K_DOC], BF16, name="doc%d" % m, tag="doc") for m in range(TILES)]
-        chat_raw = [raw.tile([P, K_CHAT], BF16, name="chat%d" % m, tag="chat") for m in range(TILES)]
-
         def rows(m):
             return slice(P * m, P * (m + 1))
 
-        def load_doc_piece(m, q, n=1):
-            cols = slice(1024 * q, 1024 * (q + n))
+        ident = keep.tile([P, P], F32, name="ident")
+        ident_bf = keep.tile([P, P], BF16, name="ident_bf")
+        vectors = keep.tile([P, P], BF16, name="vectors")
+        vector_cols = keep.tile([P, 2 * VEC_ROWS], BF16, name="vector_cols")
+        gain_all = keep.tile([P, D], BF16, name="gain_all")
+        gain_bias = keep.tile([P, D], F32, name="gain_bias")
+        u_doc = keep.tile([P, DOC_PASSES, 2 * D], U8, name="u_doc", align_bytes=256)
+        u_doc_sc = keep.tile([P, DOC_PASSES * D], U8, name="u_doc_sc", align_bytes=256)
+        u_doc_sc_by_pass = u_doc_sc[:].rearrange("p (g n) -> p g n", g=DOC_PASSES)
+        u_chat_raw = [keep.tile([P, PACK, D], BF16, name="u_chat_raw%d" % c) for c in range(CHAT_PASSES)]
+        u_chat_codes = keep.tile([P, CHAT_PASSES, D], U32, name="u_chat_codes", align_bytes=256)
+        u_chat_sc = keep.tile([P, CHAT_PASSES, D], U8, name="u_chat_sc", align_bytes=256)
+
+        doc_raw = [doc_pool.tile([P, K_DOC], BF16, name="doc%d" % m, tag="doc") for m in range(TILES)]
+        chat_raw = [chat_pool.tile([P, K_CHAT], BF16, name="chat%d" % m, tag="chat") for m in range(TILES)]
+        x_raw = [x_pool.tile([P, D], BF16, name="x%d" % m, tag="x") for m in range(TILES)]
+
+        nc.vector.memset(vectors[:], 0.0)
+        nc.vector.memset(u_doc_sc[:].bitcast(I32), 0)
+        make_identity(nc, ident[:])
+        nc.vector.tensor_copy(out=ident_bf[:], in_=ident[:])
+
+        def load_doc_slice(m, q):
+            cols = slice(SLICE * q, SLICE * (q + 1))
             nc.sync.dma_start(out=doc_raw[m][:, cols], in_=a_doc[rows(m), cols])
 
         def load_doc(m):
@@ -79,339 +92,293 @@ def tile_folded_value_attention_s1_kernel(
         def load_chat(m):
             nc.sync.dma_start(out=chat_raw[m][:], in_=a_chat[rows(m), :])
 
-        def load_ud(g, n):
-            nc.sync.dma_start(
-                out=ud[:, g : g + n, :].bitcast(I32),
-                in_=u_doc_words[g : g + n].rearrange("g p b -> p g b").bitcast(I32),
-            )
-
-        def load_uc(c):
-            nc.sync.dma_start(
-                out=uc_raw[c][:],
-                in_=u_chat[K_PASS * c : K_PASS * (c + 1), :].rearrange("(p j) n -> p j n", j=4),
-            )
-
-        x_t = {}
-
         def load_x(m):
-            x_t[m] = x_pool.tile([P, D], BF16, name="x%d" % m, tag="x")
-            nc.sync.dma_start(out=x_t[m][:], in_=x[rows(m), :])
+            nc.sync.dma_start(out=x_raw[m][:], in_=x[rows(m), :])
 
-        uds3 = uds[:].rearrange("p (g n) -> p g n", g=DOC_PASSES)
+        def load_u_doc(g):
+            nc.sync.dma_start(
+                out=u_doc[:, g : g + 2, :].bitcast(I32),
+                in_=u_doc_words[g : g + 2].rearrange("g p b -> p g b").bitcast(I32),
+            )
 
-        def load_uds(g, n):
-            for r in range(4):
-                nc.sync.dma_start(
-                    out=uds3[r:P:32, g : g + n].bitcast(I32),
-                    in_=u_doc_scales[g : g + n].rearrange("g (q r) n -> r q g n", r=4)[r].bitcast(I32),
-                )
+        def load_u_chat(c):
+            nc.sync.dma_start(
+                out=u_chat_raw[c][:],
+                in_=u_chat[K_PASS * c : K_PASS * (c + 1), :].rearrange("(p j) n -> p j n", j=PACK),
+            )
 
-        load_doc_piece(0, 0)
-        load_ud(0, 2)
-        load_uds(0, 6)
-        load_doc_piece(0, 1)
-        load_ud(2, 2)
-        load_doc_piece(0, 2)
-        load_ud(4, 2)
-        for q in range(3):
-            load_doc_piece(1, q)
-        nc.sync.dma_start(out=vec[0:8, :], in_=gain.rearrange("(c n) -> c n", n=P))
-        nc.sync.dma_start(out=vec[8:16, :], in_=bias.rearrange("(c n) -> c n", n=P))
-        load_chat(0)
-        load_chat(1)
-        load_uc(0)
-        load_doc(2)
-        load_uc(1)
-        load_chat(2)
+        load_doc_slice(0, 0)
+        nc.sync.dma_start(out=vectors[0:VEC_ROWS, :], in_=gain.rearrange("(c n) -> c n", n=P))
+        nc.sync.dma_start(out=vectors[VEC_ROWS : 2 * VEC_ROWS, :], in_=bias.rearrange("(c n) -> c n", n=P))
+        load_u_doc(0)
+        for r in range(4):
+            nc.sync.dma_start(
+                out=u_doc_sc_by_pass[r:P:32].bitcast(I32),
+                in_=u_doc_scales.rearrange("g (q r) n -> r q g n", r=4)[r].bitcast(I32),
+            )
+        load_doc_slice(0, 1)
+        load_u_doc(2)
+        load_doc_slice(0, 2)
+        load_u_doc(4)
+        for q in range(CHAT_SLICE):
+            load_doc_slice(1, q)
         load_x(0)
-        load_doc(3)
-        load_chat(3)
+        load_doc(2)
         load_x(1)
-        for m in range(4, TILES):
+        load_u_chat(0)
+        for m in range(3):
+            load_chat(m)
+        load_u_chat(1)
+        load_x(2)
+        for m in range(3, TILES):
             load_doc(m)
             load_chat(m)
-            load_x(m - 2)
-        load_x(6)
-        load_x(7)
+            load_x(m)
 
-        perm = {}
-        ready = set()
-        grp = {}
+        ordered = {}
+        in_order = set()
+        turned = {}
+        grouped = {}
         codes = {}
-        scales = {}
-        tps = {}
-        acc = {}
+        code_scales = {}
 
         def words(m, q):
-            if q < 3:
-                return doc_raw[m][:, 1024 * q : 1024 * (q + 1)].bitcast(F32)
-            return chat_raw[m][:].bitcast(F32)
+            if q == CHAT_SLICE:
+                return chat_raw[m][:].bitcast(F32)
+            return doc_raw[m][:, SLICE * q : SLICE * (q + 1)].bitcast(F32)
 
-        def prep(m, q):
-            ready.add((m, q))
-            if m not in perm:
-                perm[m] = perm_pool.tile([P, 4096], BF16, name="perm%d" % m, tag="perm")
+        def order_words(m, q):
+            if m not in ordered:
+                ordered[m] = order_pool.tile([P, SLICES * SLICE], BF16, name="ordered%d" % m, tag="ordered")
+            in_order.add((m, q))
             nc.scalar.copy(
-                out=perm[m][:, 1024 * q : 1024 * (q + 1)].bitcast(F32).rearrange("p (g u i) -> p g u i", g=2, u=2),
+                out=ordered[m][:, SLICE * q : SLICE * (q + 1)].bitcast(F32).rearrange("p (g u i) -> p g u i", g=2, u=2),
                 in_=words(m, q).rearrange("p (g i u) -> p g u i", g=2, u=2),
             )
 
-        def transpose(m, q, b):
-            t = bank(b, [P, 4, P], F32)
-            tps[m, q] = t
+        def turn(m, q, b):
+            turned[m, q] = bank(b, [P, 4, P], F32)
             for g in range(2):
                 for u in range(2):
-                    if (m, q) in ready:
-                        s = 512 * q + 256 * g + 128 * u
-                        src = perm[m][:].bitcast(F32)[:, s : s + 128]
+                    if (m, q) in in_order:
+                        first = SLICE_WORDS * q + 2 * P * g + P * u
+                        source = ordered[m][:].bitcast(F32)[:, first : first + P]
                     else:
-                        src = words(m, q)[:, 256 * g + u : 256 * (g + 1) : 2]
-                    nc.tensor.transpose(t[:, 2 * g + u, :], src, ident[:])
+                        source = words(m, q)[:, 2 * P * g + u : 2 * P * (g + 1) : 2]
+                    nc.tensor.transpose(turned[m, q][:, 2 * g + u, :], source, ident[:])
 
-        def evac(m, q):
-            if m not in grp:
-                grp[m] = grp_pool.tile([P, 4096], BF16, name="grp%d" % m, tag="grp", align_bytes=256)
-                codes[m] = a_pool.tile([P, PASSES * P], U32, name="ac%d" % m, tag="ac", align_bytes=256)
-                scales[m] = a_pool.tile([P, PASSES * P], U8, name="as%d" % m, tag="as", align_bytes=256)
+        def group(m, q):
+            if m not in grouped:
+                grouped[m] = grouped_pool.tile([P, SLICES * SLICE], BF16, name="grouped%d" % m, tag="grouped", align_bytes=256)
+                codes[m] = code_pool.tile([P, PASSES * P], U32, name="codes%d" % m, tag="codes", align_bytes=256)
+                code_scales[m] = code_pool.tile([P, PASSES * P], U8, name="scales%d" % m, tag="scales", align_bytes=256)
             nc.scalar.copy(
-                out=grp[m][:, 1024 * q : 1024 * (q + 1)].bitcast(F32).rearrange("p (g r u) -> p g r u", g=2, u=2),
-                in_=tps[m, q][:].rearrange("p (g u) r -> p g r u", u=2),
+                out=grouped[m][:, SLICE * q : SLICE * (q + 1)].bitcast(F32).rearrange("p (g r u) -> p g r u", g=2, u=2),
+                in_=turned[m, q][:].rearrange("p (g u) r -> p g r u", u=2),
             )
 
-        def quant(m, q, n=1):
-            w = slice(256 * q, 256 * (q + n))
+        def quantize(m, q, n=1):
+            w = slice(2 * P * q, 2 * P * (q + n))
             nc.vector.quantize_mx(
                 out=codes[m][:, w].bitcast(FP8X4),
-                scales=scales[m][:, w],
-                in_=grp[m][:, 1024 * q : 1024 * (q + n)],
+                scales=code_scales[m][:, w],
+                in_=grouped[m][:, SLICE * q : SLICE * (q + n)],
             )
 
-        ug = {}
+        def turn_and_quantize(m, q, b):
+            turn(m, q, b)
+            group(m, q)
+            quantize(m, q)
 
-        def uc_inter(engine, c, quarters):
-            for quarter in quarters:
-                h, part = divmod(quarter, 2)
-                if (c, h) not in ug:
-                    ug[c, h] = ug_pool.tile([P, 4 * HALF], BF16, name="ug%d%d" % (c, h), tag="ug", align_bytes=256)
-                o = ug[c, h][:, 1024 * part : 1024 * (part + 1)].rearrange("p (c i t) -> p c t i", i=4, t=4)
-                i = uc_raw[c][:, :, 256 * quarter : 256 * (quarter + 1)].rearrange("p t (c i) -> p c t i", i=4)
-                if engine == "v":
-                    nc.vector.tensor_copy(out=o, in_=i)
-                else:
-                    nc.scalar.copy(out=o, in_=i)
+        u_grouped = {}
 
-        def uc_quant(c, h):
-            w = slice(HALF * h, HALF * (h + 1))
-            nc.vector.quantize_mx(out=uc[:, c, w].bitcast(FP8X4), scales=ucs[:, c, w], in_=ug[c, h][:])
+        def group_u(copy, c, quarter):
+            h, part = divmod(quarter, 2)
+            if (c, h) not in u_grouped:
+                u_grouped[c, h] = u_grouped_pool.tile([P, PACK * HALF], BF16, name="ug%d%d" % (c, h), tag="ug", align_bytes=256)
+            width = PACK * QUARTER
+            copy(
+                out=u_grouped[c, h][:, width * part : width * (part + 1)].rearrange("p (c i t) -> p c t i", i=4, t=PACK),
+                in_=u_chat_raw[c][:, :, QUARTER * quarter : QUARTER * (quarter + 1)].rearrange("p t (c i) -> p c t i", i=4),
+            )
 
-        def open_acc(m, b):
+        def quantize_u(c, h):
+            nc.vector.quantize_mx(
+                out=u_chat_codes[:, c, HALVES[h]].bitcast(FP8X4),
+                scales=u_chat_sc[:, c, HALVES[h]],
+                in_=u_grouped[c, h][:],
+            )
+
+        sums = {}
+
+        def open_sums(m, b):
             for h in range(2):
-                acc[m, h] = bank(b + h, [P, HALF], F32)
+                sums[m, h] = bank(b + h, [P, HALF], F32)
 
-        def mm(m, g, h):
+        def multiply(m, g, cols, into):
             w = slice(P * g, P * (g + 1))
-            n = slice(HALF * h, HALF * (h + 1))
             if g < DOC_PASSES:
-                rhs = ud[:, g, 2 * HALF * h : 2 * HALF * (h + 1)].bitcast(FP4X4)
-                rhs_scale = uds3[:, g, n]
+                rhs = u_doc[:, g, 2 * cols.start : 2 * cols.stop].bitcast(FP4X4)
+                rhs_scale = u_doc_sc_by_pass[:, g, cols]
             else:
-                rhs = uc[:, g - DOC_PASSES, n].bitcast(FP8X4)
-                rhs_scale = ucs[:, g - DOC_PASSES, n]
+                rhs = u_chat_codes[:, g - DOC_PASSES, cols].bitcast(FP8X4)
+                rhs_scale = u_chat_sc[:, g - DOC_PASSES, cols]
             nc.tensor.matmul_mx(
-                out=acc[m, h][:],
+                out=into[:],
                 lhsT=codes[m][:, w].bitcast(FP8X4),
-                lhsT_scale=scales[m][:, w],
+                lhsT_scale=code_scales[m][:, w],
                 rhs=rhs,
                 rhs_scale=rhs_scale,
                 start=(g == 0),
                 stop=(g == PASSES - 1),
             )
 
-        def tail_mm(m, c, b):
-            t = bank(b, [P, P], F32)
-            acc[m, "t", c] = t
-            n = slice(HALF + P * c, HALF + P * (c + 1))
-            for g in range(PASSES):
-                w = slice(P * g, P * (g + 1))
-                if g < DOC_PASSES:
-                    rhs = ud[:, g, 2 * n.start : 2 * n.stop].bitcast(FP4X4)
-                    rhs_scale = uds3[:, g, n]
-                else:
-                    rhs = uc[:, g - DOC_PASSES, n].bitcast(FP8X4)
-                    rhs_scale = ucs[:, g - DOC_PASSES, n]
-                nc.tensor.matmul_mx(
-                    out=t[:],
-                    lhsT=codes[m][:, w].bitcast(FP8X4),
-                    lhsT_scale=scales[m][:, w],
-                    rhs=rhs,
-                    rhs_scale=rhs_scale,
-                    start=(g == 0),
-                    stop=(g == PASSES - 1),
-                )
+        def multiply_passes(m, passes):
+            for g in passes:
+                for h in range(2):
+                    multiply(m, g, HALVES[h], sums[m, h])
 
-        def tail_epi(m, c):
-            n = slice(HALF + P * c, HALF + P * (c + 1))
-            t = scaled[m]
-            nc.vector.tensor_tensor(out=t[:, n], in0=acc[m, "t", c][:], in1=gain_b[:, n], op=MULT)
-            nc.vector.tensor_tensor(out=xb[m][:, n], in0=t[:, n], in1=xb[m][:, n], op=ADD)
-
-        def mm_pass(m, g):
-            mm(m, g, 0)
-            mm(m, g, 1)
-
-        xb = {}
-
-        def residual(m):
-            xb[m] = xb_pool.tile([P, D], F32, name="xb%d" % m, tag="xb")
-            nc.vector.tensor_tensor(out=xb[m][:], in0=x_t[m][:], in1=gb[:], op=ADD)
-
+        residual = {}
         scaled = {}
 
-        def epi_mul(m, h):
-            n = slice(HALF * h, HALF * (h + 1))
-            if h == 0:
-                scaled[m] = t_pool.tile([P, D], F32, name="sc%d" % m, tag="sc")
-            nc.vector.tensor_tensor(out=scaled[m][:, n], in0=acc[m, h][:], in1=gain_b[:, n], op=MULT)
+        def make_residual(m):
+            residual[m] = residual_pool.tile([P, D], F32, name="residual%d" % m, tag="residual")
+            nc.vector.tensor_tensor(out=residual[m][:], in0=x_raw[m][:], in1=gain_bias[:], op=ADD)
 
-        def epi_add(m, h0=0, h1=2):
-            n = slice(HALF * h0, HALF * h1)
-            nc.vector.tensor_tensor(out=xb[m][:, n], in0=scaled[m][:, n], in1=xb[m][:, n], op=ADD)
+        def scale_sums(m, cols, source):
+            if m not in scaled:
+                scaled[m] = scaled_pool.tile([P, D], F32, name="scaled%d" % m, tag="scaled")
+            nc.vector.tensor_tensor(out=scaled[m][:, cols], in0=source[:], in1=gain_all[:, cols], op=MULT)
 
-        def store(m):
-            nc.sync.dma_start(out=out[rows(m), :], in_=xb[m][:])
+        def scale_both_halves(m):
+            for h in range(2):
+                scale_sums(m, HALVES[h], sums[m, h])
 
-        def store_half(m, h):
-            n = slice(HALF * h, HALF * (h + 1))
-            nc.sync.dma_start(out=out[rows(m), n], in_=xb[m][:, n])
+        def add_residual(m, cols):
+            nc.vector.tensor_tensor(out=residual[m][:, cols], in0=scaled[m][:, cols], in1=residual[m][:, cols], op=ADD)
 
-        transpose(0, 0, 6)
-        evac(0, 0)
-        quant(0, 0)
-        open_acc(0, 0)
-        mm_pass(0, 0)
-        for q, b in ((1, 7), (2, 4)):
-            transpose(0, q, b)
-            evac(0, q)
-            quant(0, q)
-        mm_pass(0, 1)
-        mm_pass(0, 2)
-        mm_pass(0, 3)
-        for q, b in ((0, 5), (1, 6), (2, 7)):
-            transpose(1, q, b)
-            evac(1, q)
-            quant(1, q)
-        vt = bank(4, [P, P], BF16)
-        nc.tensor.transpose(vt[:], vec[:], ident_bf[:])
-        nc.vector.tensor_copy(out=vcol[:], in_=vt[:, 0:16])
-        mm_pass(0, 4)
-        mm_pass(0, 5)
-        prep(0, 3)
-        prep(1, 3)
-        open_acc(1, 2)
-        mm_pass(1, 0)
-        mm_pass(1, 1)
-        transpose(0, 3, 5)
-        evac(0, 3)
-        transpose(1, 3, 6)
-        evac(1, 3)
-        uc_inter("v", 0, (0, 1))
-        uc_inter("s", 0, (3,))
-        quant(0, 3)
-        uc_inter("v", 0, (2,))
-        quant(1, 3)
-        uc_quant(0, 0)
-        uc_quant(0, 1)
-        for g in range(2, 6):
-            mm_pass(1, g)
-        for q in range(4):
-            prep(2, q)
-        uc_inter("v", 1, (0, 1))
+        def store(m, cols):
+            nc.sync.dma_start(out=out[rows(m), cols], in_=residual[m][:, cols])
+
+        ALL = slice(0, D)
+
+        def spread(first_col, b):
+            wide = bank(b, [P, D], BF16)
+            for c in range(VEC_ROWS):
+                col = vector_cols[:, first_col + c : first_col + c + 1]
+                nc.tensor.transpose(wide[:, P * c : P * (c + 1)], col.to_broadcast([P, P]), ident_bf[:])
+            return wide
+
+        vectors_t = bank(4, [P, P], BF16)
+        nc.tensor.transpose(vectors_t[:], vectors[:], ident_bf[:])
+        nc.vector.tensor_copy(out=vector_cols[:], in_=vectors_t[:, 0 : 2 * VEC_ROWS])
+        turn_and_quantize(0, 0, 6)
+        gain_wide = spread(0, 2)
+        bias_wide = spread(VEC_ROWS, 3)
+        nc.scalar.copy(out=gain_all[:], in_=gain_wide[:])
+        nc.vector.tensor_tensor(out=gain_bias[:], in0=bias_wide[:], in1=gain_all[:], op=MULT)
+
+        open_sums(0, 0)
+        turn_and_quantize(0, 1, 7)
+        multiply_passes(0, (0, 1))
+        turn_and_quantize(0, 2, 4)
+        multiply_passes(0, (2, 3))
+        for q, b in enumerate((5, 6, 7)):
+            turn_and_quantize(1, q, b)
+        multiply_passes(0, (4, 5))
+        make_residual(0)
+        open_sums(1, 2)
+        multiply_passes(1, range(4))
+        for q in range(CHAT_SLICE):
+            order_words(2, q)
+        make_residual(1)
+        group_u(nc.vector.tensor_copy, 0, 0)
+        for q, b in enumerate((6, 7, 5)):
+            turn_and_quantize(2, q, b)
+        multiply_passes(1, (4, 5))
+
+        for m, b in ((0, 6), (1, 7)):
+            turn(m, CHAT_SLICE, b)
+            group(m, CHAT_SLICE)
+        group_u(nc.scalar.copy, 0, 3)
+        group_u(nc.vector.tensor_copy, 0, 1)
+        group_u(nc.vector.tensor_copy, 0, 2)
+        quantize_u(0, 0)
+        quantize(0, CHAT_SLICE)
+        quantize(1, CHAT_SLICE)
+        quantize_u(0, 1)
+        open_sums(2, 4)
+        multiply_passes(2, range(4))
+        group_u(nc.scalar.copy, 1, 3)
+        group_u(nc.scalar.copy, 1, 2)
+        group_u(nc.vector.tensor_copy, 1, 0)
+        group_u(nc.vector.tensor_copy, 1, 1)
+        quantize_u(1, 0)
+        quantize_u(1, 1)
         for h in range(2):
             for m in range(2):
-                mm(m, 6, h)
-        for q, b in ((0, 7), (1, 5), (2, 6), (3, 7)):
-            transpose(2, q, b)
-            evac(2, q)
-        quant(2, 0)
-        uc_quant(1, 0)
-        uc_inter("v", 1, (2, 3))
-        quant(2, 1)
-        uc_quant(1, 1)
-        quant(2, 2)
-        quant(2, 3)
-        gp = bank(5, [P, D], BF16)
-        for c in range(8):
-            nc.tensor.transpose(gp[:, P * c : P * (c + 1)], vcol[:, c : c + 1].to_broadcast([P, P]), ident_bf[:])
-        bp = bank(6, [P, D], BF16)
-        for c in range(8):
-            nc.tensor.transpose(bp[:, P * c : P * (c + 1)], vcol[:, 8 + c : 9 + c].to_broadcast([P, P]), ident_bf[:])
-        nc.scalar.copy(out=gain_b[:], in_=gp[:])
-        nc.vector.tensor_tensor(out=gb[:], in0=bp[:], in1=gain_b[:], op=MULT)
-        for q in range(4):
-            prep(3, q)
-        for q in range(4):
-            prep(4, q)
-        for h in range(2):
-            for m in range(2):
-                mm(m, 7, h)
-        open_acc(2, 4)
-        for g in range(6):
-            mm_pass(2, g)
-        epi_mul(0, 0)
-        epi_mul(0, 1)
-        epi_mul(1, 0)
-        epi_mul(1, 1)
-        residual(0)
-        epi_add(0)
-        store(0)
-        residual(1)
+                multiply(m, DOC_PASSES, HALVES[h], sums[m, h])
+        turn_and_quantize(2, CHAT_SLICE, 6)
+        for q in range(SLICES):
+            order_words(3, q)
+        for m in range(2):
+            multiply_passes(m, (PASSES - 1,))
+        scale_both_halves(0)
+        scale_both_halves(1)
+        add_residual(0, ALL)
+        store(0, ALL)
 
         for m in range(2, TILES):
-            nxt = m + 1
+            ahead = m + 1
             if m > 2:
-                epi_mul(m - 1, 0)
-                epi_mul(m - 1, 1)
-            if nxt < TILES:
-                for q, b in ((0, 7), (1, 6), (2, 0), (3, 1)):
-                    transpose(nxt, q, b)
-                    evac(nxt, q)
-            if m + 3 < TILES:
-                for q in range(4):
-                    prep(m + 3, q)
+                scale_both_halves(m - 1)
+            if ahead < TILES:
+                for q, b in enumerate((7, 6, 0, 1)):
+                    turn(ahead, q, b)
+                    group(ahead, q)
+            for later in (4, 5) if m == 2 else (m + 3,):
+                if later < TILES:
+                    for q in range(SLICES):
+                        order_words(later, q)
             if m < 4:
-                quant(nxt, 0, 2)
-                quant(nxt, 2, 2)
+                for q in (0, 2):
+                    quantize(ahead, q, 2)
+                add_residual(m - 1, ALL)
                 if m == 2:
-                    residual(m)
-                epi_add(m - 1)
-                residual(nxt)
+                    make_residual(m)
+                make_residual(ahead)
             else:
-                if nxt < TILES:
-                    residual(nxt)
-                epi_add(m - 1)
-                if nxt < TILES:
-                    quant(nxt, 0, 2)
-                    quant(nxt, 2, 2)
-            store(m - 1)
+                if ahead < TILES:
+                    make_residual(ahead)
+                add_residual(m - 1, ALL)
+                if ahead < TILES:
+                    for q in (0, 2):
+                        quantize(ahead, q, 2)
+            store(m - 1, ALL)
             if m == 2:
-                mm_pass(2, 6)
-                mm_pass(2, 7)
-            elif nxt < TILES:
-                open_acc(m, 4 if m % 2 == 0 else 2)
+                multiply_passes(2, range(4, PASSES))
+            elif ahead < TILES:
+                open_sums(m, 4 if m % 2 == 0 else 2)
                 for h in range(2):
                     for g in range(PASSES):
-                        mm(m, g, h)
+                        multiply(m, g, HALVES[h], sums[m, h])
+
         last = TILES - 1
-        open_acc(last, 2)
+        first_half = bank(2, [P, HALF], F32)
         for g in range(PASSES):
-            mm(last, g, 0)
-        epi_mul(last, 0)
-        epi_add(last, 0, 1)
-        store_half(last, 0)
+            multiply(last, g, HALVES[0], first_half)
+        scale_sums(last, HALVES[0], first_half)
+        add_residual(last, HALVES[0])
+        store(last, HALVES[0])
+        narrow = []
         for c, b in enumerate((0, 1, 6, 7)):
-            tail_mm(last, c, b)
-        for c in range(4):
-            tail_epi(last, c)
+            cols = slice(HALF + P * c, HALF + P * (c + 1))
+            narrow.append((cols, bank(b, [P, P], F32)))
+            for g in range(PASSES):
+                multiply(last, g, *narrow[c])
+        for c, (cols, source) in enumerate(narrow):
+            scale_sums(last, cols, source)
+            add_residual(last, cols)
             if c == 2:
-                nc.sync.dma_start(out=out[rows(last), HALF : HALF + 3 * P], in_=xb[last][:, HALF : HALF + 3 * P])
-        nc.sync.dma_start(out=out[rows(last), D - P :], in_=xb[last][:, D - P :])
+                store(last, slice(HALF, cols.stop))
+        store(last, slice(D - P, D))

from contextlib import ExitStack

import concourse.mybir as mybir
from concourse.masks import make_identity

F32 = mybir.dt.float32
BF16 = mybir.dt.bfloat16
I32 = mybir.dt.int32
U32 = mybir.dt.uint32
U8 = mybir.dt.uint8
FP8X4 = mybir.dt.float8_e4m3fn_x4
FP4X4 = mybir.dt.float4_e2m1fn_x4
MULT = mybir.AluOpType.mult
ADD = mybir.AluOpType.add

P = 128
M, D = 1024, 1024
K_DOC, K_CHAT = 3072, 1024
PACK = 4
K_PASS = P * PACK
DOC_PASSES = K_DOC // K_PASS
CHAT_PASSES = K_CHAT // K_PASS
PASSES = DOC_PASSES + CHAT_PASSES
TILES = M // P

SLICE = 2 * K_PASS
SLICE_WORDS = SLICE // 2
SLICES = (K_DOC + K_CHAT) // SLICE
CHAT_SLICE = SLICES - 1

HALF = 512
HALVES = (slice(0, HALF), slice(HALF, D))
QUARTER = HALF // 2
VEC_ROWS = D // P

FLOPS = 2 * M * (K_DOC + K_CHAT) * D


def tile_folded_value_attention_s1_kernel(
    tc, a_doc, u_doc_words, u_doc_scales, a_chat, u_chat, bias, gain, x, out
):
    nc = tc.nc
    with ExitStack() as ctx:
        keep = ctx.enter_context(tc.tile_pool(name="keep", bufs=1))
        doc_pool = ctx.enter_context(tc.tile_pool(name="doc", bufs=TILES))
        chat_pool = ctx.enter_context(tc.tile_pool(name="chat", bufs=TILES))
        x_pool = ctx.enter_context(tc.tile_pool(name="x", bufs=TILES))
        order_pool = ctx.enter_context(tc.tile_pool(name="order", bufs=3))
        grouped_pool = ctx.enter_context(tc.tile_pool(name="grouped", bufs=3))
        code_pool = ctx.enter_context(tc.tile_pool(name="codes", bufs=4))
        u_grouped_pool = ctx.enter_context(tc.tile_pool(name="u_grouped", bufs=3))
        residual_pool = ctx.enter_context(tc.tile_pool(name="residual", bufs=4))
        scaled_pool = ctx.enter_context(tc.tile_pool(name="scaled", bufs=2))
        psum = ctx.enter_context(tc.psum_pool(name="psum", bufs=1))
        ctx.enter_context(tc.manual_schedule())

        def bank(i, shape, dtype):
            return psum.tile(shape, dtype, name="bank%d" % i, tag="bank%d" % i)

        def rows(m):
            return slice(P * m, P * (m + 1))

        ident = keep.tile([P, P], F32, name="ident")
        ident_bf = keep.tile([P, P], BF16, name="ident_bf")
        vectors = keep.tile([P, P], BF16, name="vectors")
        vector_cols = keep.tile([P, 2 * VEC_ROWS], BF16, name="vector_cols")
        gain_all = keep.tile([P, D], BF16, name="gain_all")
        gain_bias = keep.tile([P, D], F32, name="gain_bias")
        u_doc = keep.tile([P, DOC_PASSES, 2 * D], U8, name="u_doc", align_bytes=256)
        u_doc_sc = keep.tile([P, DOC_PASSES * D], U8, name="u_doc_sc", align_bytes=256)
        u_doc_sc_by_pass = u_doc_sc[:].rearrange("p (g n) -> p g n", g=DOC_PASSES)
        u_chat_raw = [keep.tile([P, PACK, D], BF16, name="u_chat_raw%d" % c) for c in range(CHAT_PASSES)]
        u_chat_codes = keep.tile([P, CHAT_PASSES, D], U32, name="u_chat_codes", align_bytes=256)
        u_chat_sc = keep.tile([P, CHAT_PASSES, D], U8, name="u_chat_sc", align_bytes=256)

        doc_raw = [doc_pool.tile([P, K_DOC], BF16, name="doc%d" % m, tag="doc") for m in range(TILES)]
        chat_raw = [chat_pool.tile([P, K_CHAT], BF16, name="chat%d" % m, tag="chat") for m in range(TILES)]
        x_raw = [x_pool.tile([P, D], BF16, name="x%d" % m, tag="x") for m in range(TILES)]

        nc.vector.memset(vectors[:], 0.0)
        nc.vector.memset(u_doc_sc[:].bitcast(I32), 0)
        make_identity(nc, ident[:])
        nc.vector.tensor_copy(out=ident_bf[:], in_=ident[:])

        def load_doc_slice(m, q):
            cols = slice(SLICE * q, SLICE * (q + 1))
            nc.sync.dma_start(out=doc_raw[m][:, cols], in_=a_doc[rows(m), cols])

        def load_doc(m):
            nc.sync.dma_start(out=doc_raw[m][:], in_=a_doc[rows(m), :])

        def load_chat(m):
            nc.sync.dma_start(out=chat_raw[m][:], in_=a_chat[rows(m), :])

        def load_x(m):
            nc.sync.dma_start(out=x_raw[m][:], in_=x[rows(m), :])

        def load_u_doc(g):
            nc.sync.dma_start(
                out=u_doc[:, g : g + 2, :].bitcast(I32),
                in_=u_doc_words[g : g + 2].rearrange("g p b -> p g b").bitcast(I32),
            )

        def load_u_chat(c):
            nc.sync.dma_start(
                out=u_chat_raw[c][:],
                in_=u_chat[K_PASS * c : K_PASS * (c + 1), :].rearrange("(p j) n -> p j n", j=PACK),
            )

        load_doc_slice(0, 0)
        nc.sync.dma_start(out=vectors[0:VEC_ROWS, :], in_=gain.rearrange("(c n) -> c n", n=P))
        nc.sync.dma_start(out=vectors[VEC_ROWS : 2 * VEC_ROWS, :], in_=bias.rearrange("(c n) -> c n", n=P))
        load_u_doc(0)
        for r in range(4):
            nc.sync.dma_start(
                out=u_doc_sc_by_pass[r:P:32].bitcast(I32),
                in_=u_doc_scales.rearrange("g (q r) n -> r q g n", r=4)[r].bitcast(I32),
            )
        load_doc_slice(0, 1)
        load_u_doc(2)
        load_doc_slice(0, 2)
        load_u_doc(4)
        for q in range(CHAT_SLICE):
            load_doc_slice(1, q)
        load_x(0)
        load_doc(2)
        load_x(1)
        load_u_chat(0)
        for m in range(3):
            load_chat(m)
        load_u_chat(1)
        load_x(2)
        for m in range(3, TILES):
            load_doc(m)
            load_chat(m)
            load_x(m)

        ordered = {}
        in_order = set()
        turned = {}
        grouped = {}
        codes = {}
        code_scales = {}

        def words(m, q):
            if q == CHAT_SLICE:
                return chat_raw[m][:].bitcast(F32)
            return doc_raw[m][:, SLICE * q : SLICE * (q + 1)].bitcast(F32)

        def order_words(m, q):
            if m not in ordered:
                ordered[m] = order_pool.tile([P, SLICES * SLICE], BF16, name="ordered%d" % m, tag="ordered")
            in_order.add((m, q))
            nc.scalar.copy(
                out=ordered[m][:, SLICE * q : SLICE * (q + 1)].bitcast(F32).rearrange("p (g u i) -> p g u i", g=2, u=2),
                in_=words(m, q).rearrange("p (g i u) -> p g u i", g=2, u=2),
            )

        def turn(m, q, b):
            turned[m, q] = bank(b, [P, 4, P], F32)
            for g in range(2):
                for u in range(2):
                    if (m, q) in in_order:
                        first = SLICE_WORDS * q + 2 * P * g + P * u
                        source = ordered[m][:].bitcast(F32)[:, first : first + P]
                    else:
                        source = words(m, q)[:, 2 * P * g + u : 2 * P * (g + 1) : 2]
                    nc.tensor.transpose(turned[m, q][:, 2 * g + u, :], source, ident[:])

        def group(m, q):
            if m not in grouped:
                grouped[m] = grouped_pool.tile([P, SLICES * SLICE], BF16, name="grouped%d" % m, tag="grouped", align_bytes=256)
                codes[m] = code_pool.tile([P, PASSES * P], U32, name="codes%d" % m, tag="codes", align_bytes=256)
                code_scales[m] = code_pool.tile([P, PASSES * P], U8, name="scales%d" % m, tag="scales", align_bytes=256)
            nc.scalar.copy(
                out=grouped[m][:, SLICE * q : SLICE * (q + 1)].bitcast(F32).rearrange("p (g r u) -> p g r u", g=2, u=2),
                in_=turned[m, q][:].rearrange("p (g u) r -> p g r u", u=2),
            )

        def quantize(m, q, n=1):
            w = slice(2 * P * q, 2 * P * (q + n))
            nc.vector.quantize_mx(
                out=codes[m][:, w].bitcast(FP8X4),
                scales=code_scales[m][:, w],
                in_=grouped[m][:, SLICE * q : SLICE * (q + n)],
            )

        def turn_and_quantize(m, q, b):
            turn(m, q, b)
            group(m, q)
            quantize(m, q)

        u_grouped = {}

        def group_u(copy, c, quarter):
            h, part = divmod(quarter, 2)
            if (c, h) not in u_grouped:
                u_grouped[c, h] = u_grouped_pool.tile([P, PACK * HALF], BF16, name="ug%d%d" % (c, h), tag="ug", align_bytes=256)
            width = PACK * QUARTER
            copy(
                out=u_grouped[c, h][:, width * part : width * (part + 1)].rearrange("p (c i t) -> p c t i", i=4, t=PACK),
                in_=u_chat_raw[c][:, :, QUARTER * quarter : QUARTER * (quarter + 1)].rearrange("p t (c i) -> p c t i", i=4),
            )

        def quantize_u(c, h):
            nc.vector.quantize_mx(
                out=u_chat_codes[:, c, HALVES[h]].bitcast(FP8X4),
                scales=u_chat_sc[:, c, HALVES[h]],
                in_=u_grouped[c, h][:],
            )

        sums = {}

        def open_sums(m, b):
            for h in range(2):
                sums[m, h] = bank(b + h, [P, HALF], F32)

        def multiply(m, g, cols, into):
            w = slice(P * g, P * (g + 1))
            if g < DOC_PASSES:
                rhs = u_doc[:, g, 2 * cols.start : 2 * cols.stop].bitcast(FP4X4)
                rhs_scale = u_doc_sc_by_pass[:, g, cols]
            else:
                rhs = u_chat_codes[:, g - DOC_PASSES, cols].bitcast(FP8X4)
                rhs_scale = u_chat_sc[:, g - DOC_PASSES, cols]
            nc.tensor.matmul_mx(
                out=into[:],
                lhsT=codes[m][:, w].bitcast(FP8X4),
                lhsT_scale=code_scales[m][:, w],
                rhs=rhs,
                rhs_scale=rhs_scale,
                start=(g == 0),
                stop=(g == PASSES - 1),
            )

        def multiply_passes(m, passes):
            for g in passes:
                for h in range(2):
                    multiply(m, g, HALVES[h], sums[m, h])

        residual = {}
        scaled = {}

        def make_residual(m):
            residual[m] = residual_pool.tile([P, D], F32, name="residual%d" % m, tag="residual")
            nc.vector.tensor_tensor(out=residual[m][:], in0=x_raw[m][:], in1=gain_bias[:], op=ADD)

        def scale_sums(m, cols, source):
            if m not in scaled:
                scaled[m] = scaled_pool.tile([P, D], F32, name="scaled%d" % m, tag="scaled")
            nc.vector.tensor_tensor(out=scaled[m][:, cols], in0=source[:], in1=gain_all[:, cols], op=MULT)

        def scale_both_halves(m):
            for h in range(2):
                scale_sums(m, HALVES[h], sums[m, h])

        def add_residual(m, cols):
            nc.vector.tensor_tensor(out=residual[m][:, cols], in0=scaled[m][:, cols], in1=residual[m][:, cols], op=ADD)

        def store(m, cols):
            nc.sync.dma_start(out=out[rows(m), cols], in_=residual[m][:, cols])

        ALL = slice(0, D)

        def spread(first_col, b):
            wide = bank(b, [P, D], BF16)
            for c in range(VEC_ROWS):
                col = vector_cols[:, first_col + c : first_col + c + 1]
                nc.tensor.transpose(wide[:, P * c : P * (c + 1)], col.to_broadcast([P, P]), ident_bf[:])
            return wide

        vectors_t = bank(4, [P, P], BF16)
        nc.tensor.transpose(vectors_t[:], vectors[:], ident_bf[:])
        nc.vector.tensor_copy(out=vector_cols[:], in_=vectors_t[:, 0 : 2 * VEC_ROWS])
        turn_and_quantize(0, 0, 6)
        gain_wide = spread(0, 2)
        bias_wide = spread(VEC_ROWS, 3)
        nc.scalar.copy(out=gain_all[:], in_=gain_wide[:])
        nc.vector.tensor_tensor(out=gain_bias[:], in0=bias_wide[:], in1=gain_all[:], op=MULT)

        open_sums(0, 0)
        turn_and_quantize(0, 1, 7)
        multiply_passes(0, (0, 1))
        turn_and_quantize(0, 2, 4)
        multiply_passes(0, (2, 3))
        for q, b in enumerate((5, 6, 7)):
            turn_and_quantize(1, q, b)
        multiply_passes(0, (4, 5))
        make_residual(0)
        open_sums(1, 2)
        multiply_passes(1, range(4))
        for q in range(CHAT_SLICE):
            order_words(2, q)
        make_residual(1)
        group_u(nc.vector.tensor_copy, 0, 0)
        for q, b in enumerate((6, 7, 5)):
            turn_and_quantize(2, q, b)
        multiply_passes(1, (4, 5))

        for m, b in ((0, 6), (1, 7)):
            turn(m, CHAT_SLICE, b)
            group(m, CHAT_SLICE)
        group_u(nc.scalar.copy, 0, 3)
        group_u(nc.vector.tensor_copy, 0, 1)
        group_u(nc.vector.tensor_copy, 0, 2)
        quantize_u(0, 0)
        quantize(0, CHAT_SLICE)
        quantize(1, CHAT_SLICE)
        quantize_u(0, 1)
        open_sums(2, 4)
        multiply_passes(2, range(4))
        group_u(nc.scalar.copy, 1, 3)
        group_u(nc.scalar.copy, 1, 2)
        group_u(nc.vector.tensor_copy, 1, 0)
        group_u(nc.vector.tensor_copy, 1, 1)
        quantize_u(1, 0)
        quantize_u(1, 1)
        for h in range(2):
            for m in range(2):
                multiply(m, DOC_PASSES, HALVES[h], sums[m, h])
        turn_and_quantize(2, CHAT_SLICE, 6)
        for q in range(SLICES):
            order_words(3, q)
        for m in range(2):
            multiply_passes(m, (PASSES - 1,))
        scale_both_halves(0)
        scale_both_halves(1)
        add_residual(0, ALL)
        store(0, ALL)

        for m in range(2, TILES):
            ahead = m + 1
            if m > 2:
                scale_both_halves(m - 1)
            if ahead < TILES:
                for q, b in enumerate((7, 6, 0, 1)):
                    turn(ahead, q, b)
                    group(ahead, q)
            for later in (4, 5) if m == 2 else (m + 3,):
                if later < TILES:
                    for q in range(SLICES):
                        order_words(later, q)
            if m < 4:
                for q in (0, 2):
                    quantize(ahead, q, 2)
                add_residual(m - 1, ALL)
                if m == 2:
                    make_residual(m)
                make_residual(ahead)
            else:
                if ahead < TILES:
                    make_residual(ahead)
                add_residual(m - 1, ALL)
                if ahead < TILES:
                    for q in (0, 2):
                        quantize(ahead, q, 2)
            store(m - 1, ALL)
            if m == 2:
                multiply_passes(2, range(4, PASSES))
            elif ahead < TILES:
                open_sums(m, 4 if m % 2 == 0 else 2)
                for h in range(2):
                    for g in range(PASSES):
                        multiply(m, g, HALVES[h], sums[m, h])

        last = TILES - 1
        first_half = bank(2, [P, HALF], F32)
        for g in range(PASSES):
            multiply(last, g, HALVES[0], first_half)
        scale_sums(last, HALVES[0], first_half)
        add_residual(last, HALVES[0])
        store(last, HALVES[0])
        narrow = []
        for c, b in enumerate((0, 1, 6, 7)):
            cols = slice(HALF + P * c, HALF + P * (c + 1))
            narrow.append((cols, bank(b, [P, P], F32)))
            for g in range(PASSES):
                multiply(last, g, *narrow[c])
        for c, (cols, source) in enumerate(narrow):
            scale_sums(last, cols, source)
            add_residual(last, cols)
            if c == 2:
                store(last, slice(HALF, cols.stop))
        store(last, slice(D - P, D))
